import numpy as np
CORES = [93,349,221,477]
N = 4
def setup_inputs(rng):
    return {"x1": rng.standard_normal((N, 128, 128), dtype=np.float32), "x2": rng.standard_normal((N, 128, 1), dtype=np.float32), "x3": rng.standard_normal((N, 128, 512), dtype=np.float32), "x4": rng.standard_normal((N, 128, 32), dtype=np.float32)}
def reference(x1, x2, x3, x4):
    out = {}
    s = x1.sum(axis=0, dtype=np.float64).astype(x1.dtype)
    out["y1"] = np.broadcast_to(s, (N,) + s.shape)
    s = x2.sum(axis=0, dtype=np.float64).astype(x2.dtype)
    out["y2"] = np.broadcast_to(s, (N,) + s.shape)
    s = x3.sum(axis=0, dtype=np.float64).astype(x3.dtype)
    out["y3"] = np.broadcast_to(s, (N,) + s.shape)
    s = x4.sum(axis=0, dtype=np.float64).astype(x4.dtype)
    out["y4"] = np.broadcast_to(s, (N,) + s.shape)
    return out

@@ -1,0 +1,99 @@
+from concourse.bass import DstId, RemoteDMATransfer
+
+NSLOT = 11
+SCRATCH = {
+    "a": ("dram", [NSLOT, 128, 64], "float32"),
+    "b": ("dram", [NSLOT, 128, 64], "float32"),
+    "c": ("dram", [NSLOT, 128, 64], "float32"),
+}
+SEMAPHORES = ["ldx", "lds", "s1", "s2", "ls", "rxa", "rxb", "rs", "st"]
+
+RACK, CABLE = 0, 1
+RANK_CORE = 5
+SLOTS = [
+    (6, RACK, 0, 1), (6, RACK, 1, 1), (2, RACK, 2, 1), (2, RACK, 3, 1),
+    (7, CABLE, 4, 1), (7, CABLE, 5, 1), (0, CABLE, 6, 1), (0, CABLE, 7, 1),
+    (1, RACK, 0, 2), (3, CABLE, 2, 2), (4, RACK, 4, 4),
+]
+WAVES = (range(0, 8), range(8, 11))
+
+
+def bits(lo, n):
+    return ((1 << n) - 1) << lo
+
+
+def partner(h, kind):
+    return h ^ 1 if kind == RACK else 3 - h
+
+
+def dst_id(topo, dst, src):
+    rid, pid = topo.addr(dst, src)
+    return DstId(rid=rid, pnc=pid)
+
+
+def rank_side(g, core, T, topo):
+    s = T.sem
+    h = topo.host(core)
+    chip0 = core % 128 - core % 8
+    g.sync.dma_start(T.a[0:4], T.x3[0:64, :]).then_inc(s.ldx, 16)
+    g.scalar.dma_start(T.a[4:8], T.x3[64:128, :]).then_inc(s.ldx, 16)
+    g.sync.dma_start(T.a[8:10], T.x1[:]).then_inc(s.lds, 16)
+    g.scalar.dma_start(T.a[10, 0:64, :], T.x4[:]).then_inc(s.lds, 16)
+    g.scalar.dma_start(T.a[10, 64:66, :], T.x2[:]).then_inc(s.lds, 16)
+    g.sync.dma_start(T.a[10, 66:128, :], T.x1[0:31, :]).then_inc(s.lds, 16)
+    sent = 0
+    for wave, sem, val in ((WAVES[0], s.ldx, 32), (WAVES[1], s.lds, 64)):
+        g.wait_ge(sem, val)
+        trs = []
+        for t in wave:
+            k, kind, lo, n = SLOTS[t]
+            far = partner(h, kind) * 128 + chip0 + k
+            near = h * 128 + chip0 + k
+            trs.append(RemoteDMATransfer(dst_ids=[dst_id(topo, far, core)], dma_engine_mask=bits(lo, n),
+                                         remote_sem=s.s1, src=T.a[t], dst=T.b[t], alu_op=0))
+            trs.append(RemoteDMATransfer(dst_ids=[dst_id(topo, near, core)], dma_engine_mask=bits(8 + lo, n),
+                                         remote_sem=s.s1, src=T.a[t], dst=T.a[t], alu_op=0))
+            sent += 2 * n
+        g.remote_dma_fused(trs, local_sem=s.ls)
+    g.sync.wait_ge(s.rxa, 32)
+    g.sync.dma_start(T.y3[0:64, :], T.c[0:4]).then_inc(s.st, 16)
+    g.scalar.wait_ge(s.rxb, 32)
+    g.scalar.dma_start(T.y3[64:128, :], T.c[4:8]).then_inc(s.st, 16)
+    g.sync.wait_ge(s.rs, 48)
+    g.sync.dma_start(T.y1[:], T.c[8:10]).then_inc(s.st, 16)
+    g.scalar.wait_ge(s.rs, 48)
+    g.scalar.dma_start(T.y4[:], T.c[10, 0:64, :]).then_inc(s.st, 16)
+    g.scalar.dma_start(T.y2[:], T.c[10, 64:66, :]).then_inc(s.st, 16)
+    g.wait_ge(s.ls, sent)
+    g.wait_ge(s.st, 80)
+
+
+def helper_side(g, core, T, topo):
+    s = T.sem
+    h = topo.host(core)
+    k = core % 8
+    mine = [t for t in range(NSLOT) if SLOTS[t][0] == k]
+    if not mine:
+        return
+    kind = SLOTS[mine[0]][1]
+    g.wait_ge(s.s1, sum(2 * SLOTS[t][3] for t in mine))
+    peer = dst_id(topo, partner(h, 1 - kind) * 128 + core % 128, core)
+    e = 8 // len(mine)
+    g.remote_dma_fused([RemoteDMATransfer(dst_ids=[peer], dma_engine_mask=bits(i * e, e), remote_sem=s.s2,
+                                          srcs=[T.a[t], T.b[t]], dsts=[T.c[t]], alu_op=1)
+                        for i, t in enumerate(mine)], local_sem=s.ls)
+    g.wait_ge(s.s2, 8)
+    home = dst_id(topo, core - k + RANK_CORE, core)
+    done = s.rs if mine[0] >= 8 else (s.rxa if kind == RACK else s.rxb)
+    e = 16 // len(mine)
+    g.remote_dma_fused([RemoteDMATransfer(dst_ids=[home], dma_engine_mask=bits(i * e, e), remote_sem=done,
+                                          srcs=[T.a[t], T.b[t], T.c[t]], dsts=[T.c[t]], alu_op=1)
+                        for i, t in enumerate(mine)], local_sem=s.ls)
+    g.wait_ge(s.ls, 24)
+
+
+def rank_program(g, core, T, topo):
+    if T.rank_of(core) is not None:
+        rank_side(g, core, T, topo)
+    elif topo.chip(core) == topo.chip(T.cores[0]):
+        helper_side(g, core, T, topo)

@@ -11,11 +11,12 @@ SEMAPHORES = ["ldx", "lds", "s1", "s2", "ls", "rxa", "rxb", "rs", "st"]
 RACK, CABLE = 0, 1
 RANK_CORE = 5
 SLOTS = [
-    (6, RACK, 0, 1), (6, RACK, 1, 1), (2, RACK, 2, 1), (2, RACK, 3, 1),
-    (7, CABLE, 4, 1), (7, CABLE, 5, 1), (0, CABLE, 6, 1), (0, CABLE, 7, 1),
-    (1, RACK, 0, 2), (3, CABLE, 2, 2), (4, RACK, 4, 4),
+    (RACK, (0, 3), 0), (RACK, (0, 3), 6), (RACK, (1, 2), 0), (RACK, (1, 2), 6),
+    (CABLE, (0, 1), 1), (CABLE, (0, 1), 7), (CABLE, (2, 3), 1), (CABLE, (2, 3), 7),
+    (RACK, (0, 3), 2), (RACK, (1, 2), 2),
+    (CABLE, (0, 1), 3),
 ]
-WAVES = (range(0, 8), range(8, 11))
+WAVES = ((range(0, 8), 2), (range(8, 11), 4))
 
 
 def bits(lo, n):
@@ -42,26 +43,31 @@ def rank_side(g, core, T, topo):
     g.scalar.dma_start(T.a[10, 64:66, :], T.x2[:]).then_inc(s.lds, 16)
     g.sync.dma_start(T.a[10, 66:128, :], T.x1[0:31, :]).then_inc(s.lds, 16)
     sent = 0
-    for wave, sem, val in ((WAVES[0], s.ldx, 32), (WAVES[1], s.lds, 64)):
+    for (wave, n), sem, val in ((WAVES[0], s.ldx, 32), (WAVES[1], s.lds, 64)):
         g.wait_ge(sem, val)
         trs = []
+        near_lo, far_lo = 8, 0
         for t in wave:
-            k, kind, lo, n = SLOTS[t]
-            far = partner(h, kind) * 128 + chip0 + k
-            near = h * 128 + chip0 + k
-            trs.append(RemoteDMATransfer(dst_ids=[dst_id(topo, far, core)], dma_engine_mask=bits(lo, n),
-                                         remote_sem=s.s1, src=T.a[t], dst=T.b[t], alu_op=0))
-            trs.append(RemoteDMATransfer(dst_ids=[dst_id(topo, near, core)], dma_engine_mask=bits(8 + lo, n),
-                                         remote_sem=s.s1, src=T.a[t], dst=T.a[t], alu_op=0))
-            sent += 2 * n
+            kind, owners, k = SLOTS[t]
+            if h in owners:
+                trs.append(RemoteDMATransfer(dst_ids=[dst_id(topo, h * 128 + chip0 + k, core)],
+                                             dma_engine_mask=bits(near_lo, n), remote_sem=s.s1,
+                                             src=T.a[t], dst=T.a[t], alu_op=0))
+                near_lo += n
+            else:
+                trs.append(RemoteDMATransfer(dst_ids=[dst_id(topo, partner(h, kind) * 128 + chip0 + k, core)],
+                                             dma_engine_mask=bits(far_lo, n), remote_sem=s.s1,
+                                             src=T.a[t], dst=T.b[t], alu_op=0))
+                far_lo += n
+            sent += n
         g.remote_dma_fused(trs, local_sem=s.ls)
     g.sync.wait_ge(s.rxa, 32)
     g.sync.dma_start(T.y3[0:64, :], T.c[0:4]).then_inc(s.st, 16)
     g.scalar.wait_ge(s.rxb, 32)
     g.scalar.dma_start(T.y3[64:128, :], T.c[4:8]).then_inc(s.st, 16)
-    g.sync.wait_ge(s.rs, 48)
+    g.sync.wait_ge(s.rs, 24)
     g.sync.dma_start(T.y1[:], T.c[8:10]).then_inc(s.st, 16)
-    g.scalar.wait_ge(s.rs, 48)
+    g.scalar.wait_ge(s.rs, 24)
     g.scalar.dma_start(T.y4[:], T.c[10, 0:64, :]).then_inc(s.st, 16)
     g.scalar.dma_start(T.y2[:], T.c[10, 64:66, :]).then_inc(s.st, 16)
     g.wait_ge(s.ls, sent)
@@ -72,23 +78,24 @@ def helper_side(g, core, T, topo):
     s = T.sem
     h = topo.host(core)
     k = core % 8
-    mine = [t for t in range(NSLOT) if SLOTS[t][0] == k]
+    mine = [t for t in range(NSLOT) if SLOTS[t][2] == k and h in SLOTS[t][1]]
     if not mine:
         return
-    kind = SLOTS[mine[0]][1]
-    g.wait_ge(s.s1, sum(2 * SLOTS[t][3] for t in mine))
+    t = mine[0]
+    kind = SLOTS[t][0]
+    n = WAVES[0][1] if t in WAVES[0][0] else WAVES[1][1]
+    g.wait_ge(s.s1, 2 * n)
     peer = dst_id(topo, partner(h, 1 - kind) * 128 + core % 128, core)
-    e = 8 // len(mine)
-    g.remote_dma_fused([RemoteDMATransfer(dst_ids=[peer], dma_engine_mask=bits(i * e, e), remote_sem=s.s2,
-                                          srcs=[T.a[t], T.b[t]], dsts=[T.c[t]], alu_op=1)
-                        for i, t in enumerate(mine)], local_sem=s.ls)
+    g.remote_dma_fused([RemoteDMATransfer(dst_ids=[peer], dma_engine_mask=bits(0, 8), remote_sem=s.s2,
+                                          srcs=[T.a[t], T.b[t]], dsts=[T.c[t]], alu_op=1)], local_sem=s.ls)
     g.wait_ge(s.s2, 8)
     home = dst_id(topo, core - k + RANK_CORE, core)
-    done = s.rs if mine[0] >= 8 else (s.rxa if kind == RACK else s.rxb)
-    e = 16 // len(mine)
-    g.remote_dma_fused([RemoteDMATransfer(dst_ids=[home], dma_engine_mask=bits(i * e, e), remote_sem=done,
-                                          srcs=[T.a[t], T.b[t], T.c[t]], dsts=[T.c[t]], alu_op=1)
-                        for i, t in enumerate(mine)], local_sem=s.ls)
+    away = dst_id(topo, partner(h, kind) * 128 + core % 128 - k + RANK_CORE, core)
+    done = s.rs if t >= 8 else (s.rxa if kind == RACK else s.rxb)
+    g.remote_dma_fused([RemoteDMATransfer(dst_ids=[away], dma_engine_mask=bits(0, 8), remote_sem=done,
+                                          srcs=[T.a[t], T.b[t], T.c[t]], dsts=[T.c[t]], alu_op=1),
+                        RemoteDMATransfer(dst_ids=[home], dma_engine_mask=bits(8, 8), remote_sem=done,
+                                          srcs=[T.a[t], T.b[t], T.c[t]], dsts=[T.c[t]], alu_op=1)], local_sem=s.ls)
     g.wait_ge(s.ls, 24)
 
 

@@ -6,7 +6,7 @@ SCRATCH = {
     "b": ("dram", [NSLOT, 128, 64], "float32"),
     "c": ("dram", [NSLOT, 128, 64], "float32"),
 }
-SEMAPHORES = ["ldx", "lds", "s1", "s2", "ls", "rxa", "rxb", "rs", "st"]
+SEMAPHORES = ["ld1", "ld2", "s1", "s2", "ls", "r0", "r1", "r2", "r3", "rs", "st"]
 
 RACK, CABLE = 0, 1
 RANK_CORE = 5
@@ -16,7 +16,6 @@ SLOTS = [
     (RACK, (0, 3), 2), (RACK, (1, 2), 2),
     (CABLE, (0, 1), 3),
 ]
-WAVES = ((range(0, 8), 2), (range(8, 11), 4))
 
 
 def bits(lo, n):
@@ -25,6 +24,14 @@ def bits(lo, n):
 
 def partner(h, kind):
     return h ^ 1 if kind == RACK else 3 - h
+
+
+def owns(h, t):
+    return h in SLOTS[t][1]
+
+
+def engines(h, t):
+    return 4 if t in (8, 9) and not owns(h, t) else 2
 
 
 def dst_id(topo, dst, src):
@@ -36,62 +43,77 @@ def rank_side(g, core, T, topo):
     s = T.sem
     h = topo.host(core)
     chip0 = core % 128 - core % 8
-    g.sync.dma_start(T.a[0:4], T.x3[0:64, :]).then_inc(s.ldx, 16)
-    g.scalar.dma_start(T.a[4:8], T.x3[64:128, :]).then_inc(s.ldx, 16)
-    g.sync.dma_start(T.a[8:10], T.x1[:]).then_inc(s.lds, 16)
-    g.scalar.dma_start(T.a[10, 0:64, :], T.x4[:]).then_inc(s.lds, 16)
-    g.scalar.dma_start(T.a[10, 64:66, :], T.x2[:]).then_inc(s.lds, 16)
-    g.sync.dma_start(T.a[10, 66:128, :], T.x1[0:31, :]).then_inc(s.lds, 16)
-    sent = 0
-    for (wave, n), sem, val in ((WAVES[0], s.ldx, 32), (WAVES[1], s.lds, 64)):
-        g.wait_ge(sem, val)
-        trs = []
-        near_lo, far_lo = 8, 0
-        for t in wave:
-            kind, owners, k = SLOTS[t]
-            if h in owners:
-                trs.append(RemoteDMATransfer(dst_ids=[dst_id(topo, h * 128 + chip0 + k, core)],
-                                             dma_engine_mask=bits(near_lo, n), remote_sem=s.s1,
-                                             src=T.a[t], dst=T.a[t], alu_op=0))
-                near_lo += n
-            else:
-                trs.append(RemoteDMATransfer(dst_ids=[dst_id(topo, partner(h, kind) * 128 + chip0 + k, core)],
-                                             dma_engine_mask=bits(far_lo, n), remote_sem=s.s1,
-                                             src=T.a[t], dst=T.b[t], alu_op=0))
-                far_lo += n
-            sent += n
-        g.remote_dma_fused(trs, local_sem=s.ls)
-    g.sync.wait_ge(s.rxa, 32)
-    g.sync.dma_start(T.y3[0:64, :], T.c[0:4]).then_inc(s.st, 16)
-    g.scalar.wait_ge(s.rxb, 32)
-    g.scalar.dma_start(T.y3[64:128, :], T.c[4:8]).then_inc(s.st, 16)
+    queues = ((g.sync, (0, 1)), (g.scalar, (2, 3)))
+
+    def piece(j):
+        return slice(2 * j, 2 * j + 2), slice(32 * j, 32 * j + 32)
+
+    for q, js in queues:
+        for j in js:
+            if not owns(h, 2 * j):
+                sl, rows = piece(j)
+                q.dma_start(T.a[sl], T.x3[rows, :]).then_inc(s.ld1, 16)
+    g.sync.dma_start(T.a[8:10], T.x1[:]).then_inc(s.ld2, 16)
+    g.scalar.dma_start(T.a[10, 0:64, :], T.x4[:]).then_inc(s.ld2, 16)
+    g.scalar.dma_start(T.a[10, 64:66, :], T.x2[:]).then_inc(s.ld2, 16)
+    g.sync.dma_start(T.a[10, 66:128, :], T.x1[0:31, :]).then_inc(s.ld2, 16)
+    for q, js in queues:
+        for j in js:
+            if owns(h, 2 * j):
+                sl, rows = piece(j)
+                q.dma_start(T.a[sl], T.x3[rows, :]).then_inc(s.ld2, 16)
+
+    def hand(t, lo):
+        kind, owners, k = SLOTS[t]
+        n = engines(h, t)
+        if owns(h, t):
+            return RemoteDMATransfer(dst_ids=[dst_id(topo, h * 128 + chip0 + k, core)], dma_engine_mask=bits(lo, n),
+                                     remote_sem=s.s1, src=T.a[t], dst=T.a[t], alu_op=0)
+        return RemoteDMATransfer(dst_ids=[dst_id(topo, partner(h, kind) * 128 + chip0 + k, core)],
+                                 dma_engine_mask=bits(lo, n), remote_sem=s.s1, src=T.a[t], dst=T.b[t], alu_op=0)
+
+    g.wait_ge(s.ld1, 32)
+    g.remote_dma_fused([hand(t, 2 * i) for i, t in enumerate(t for t in range(8) if not owns(h, t))], local_sem=s.ls)
+    g.wait_ge(s.ld2, 96)
+    trs = [hand(t, 8 + 2 * i) for i, t in enumerate(t for t in range(8) if owns(h, t))]
+    lo = 0
+    for t in (8, 9, 10):
+        trs.append(hand(t, lo))
+        lo += engines(h, t)
+    g.remote_dma_fused(trs, local_sem=s.ls)
+
+    for q, js in queues:
+        for j in sorted(js, key=lambda j: not owns(h, 2 * j)):
+            sl, rows = piece(j)
+            q.wait_ge(s["r%d" % j], 16)
+            q.dma_start(T.y3[rows, :], T.c[sl]).then_inc(s.st, 16)
     g.sync.wait_ge(s.rs, 24)
     g.sync.dma_start(T.y1[:], T.c[8:10]).then_inc(s.st, 16)
     g.scalar.wait_ge(s.rs, 24)
     g.scalar.dma_start(T.y4[:], T.c[10, 0:64, :]).then_inc(s.st, 16)
     g.scalar.dma_start(T.y2[:], T.c[10, 64:66, :]).then_inc(s.st, 16)
-    g.wait_ge(s.ls, sent)
-    g.wait_ge(s.st, 80)
+    g.wait_ge(s.ls, 8 + 8 + 8)
+    g.wait_ge(s.st, 7 * 16)
 
 
 def helper_side(g, core, T, topo):
     s = T.sem
     h = topo.host(core)
     k = core % 8
-    mine = [t for t in range(NSLOT) if SLOTS[t][2] == k and h in SLOTS[t][1]]
+    mine = [t for t in range(NSLOT) if SLOTS[t][2] == k and owns(h, t)]
     if not mine:
         return
     t = mine[0]
     kind = SLOTS[t][0]
-    n = WAVES[0][1] if t in WAVES[0][0] else WAVES[1][1]
-    g.wait_ge(s.s1, 2 * n)
-    peer = dst_id(topo, partner(h, 1 - kind) * 128 + core % 128, core)
+    first, second = partner(h, kind), partner(h, 1 - kind)
+    g.wait_ge(s.s1, engines(h, t) + engines(first, t))
+    peer = dst_id(topo, second * 128 + core % 128, core)
     g.remote_dma_fused([RemoteDMATransfer(dst_ids=[peer], dma_engine_mask=bits(0, 8), remote_sem=s.s2,
                                           srcs=[T.a[t], T.b[t]], dsts=[T.c[t]], alu_op=1)], local_sem=s.ls)
     g.wait_ge(s.s2, 8)
     home = dst_id(topo, core - k + RANK_CORE, core)
-    away = dst_id(topo, partner(h, kind) * 128 + core % 128 - k + RANK_CORE, core)
-    done = s.rs if t >= 8 else (s.rxa if kind == RACK else s.rxb)
+    away = dst_id(topo, first * 128 + core % 128 - k + RANK_CORE, core)
+    done = s.rs if t >= 8 else s["r%d" % (t // 2)]
     g.remote_dma_fused([RemoteDMATransfer(dst_ids=[away], dma_engine_mask=bits(0, 8), remote_sem=done,
                                           srcs=[T.a[t], T.b[t], T.c[t]], dsts=[T.c[t]], alu_op=1),
                         RemoteDMATransfer(dst_ids=[home], dma_engine_mask=bits(8, 8), remote_sem=done,

@@ -1,21 +1,22 @@
 from concourse.bass import DstId, RemoteDMATransfer
 
-NSLOT = 11
+NSLOT = 22
 SCRATCH = {
-    "a": ("dram", [NSLOT, 128, 64], "float32"),
-    "b": ("dram", [NSLOT, 128, 64], "float32"),
-    "c": ("dram", [NSLOT, 128, 64], "float32"),
+    "a": ("dram", [NSLOT, 128, 32], "float32"),
+    "b": ("dram", [NSLOT, 128, 32], "float32"),
+    "c": ("dram", [NSLOT, 128, 32], "float32"),
 }
 SEMAPHORES = ["ld1", "ld2", "s1", "s2", "ls", "r0", "r1", "r2", "r3", "rs", "st"]
 
 RACK, CABLE = 0, 1
 RANK_CORE = 5
-SLOTS = [
-    (RACK, (0, 3), 0), (RACK, (0, 3), 6), (RACK, (1, 2), 0), (RACK, (1, 2), 6),
-    (CABLE, (0, 1), 1), (CABLE, (0, 1), 7), (CABLE, (2, 3), 1), (CABLE, (2, 3), 7),
-    (RACK, (0, 3), 2), (RACK, (1, 2), 2),
-    (CABLE, (0, 1), 3),
-]
+NX = 16
+SLOTS = (
+    [(RACK, (0, 3), 0)] * 2 + [(RACK, (0, 3), 6)] * 2 + [(RACK, (1, 2), 0)] * 2 + [(RACK, (1, 2), 6)] * 2
+    + [(CABLE, (0, 1), 1)] * 2 + [(CABLE, (0, 1), 7)] * 2 + [(CABLE, (2, 3), 1)] * 2 + [(CABLE, (2, 3), 7)] * 2
+    + [(RACK, (0, 3), 2), (RACK, (1, 2), 2), (CABLE, (0, 1), 3), (CABLE, (2, 3), 3)]
+    + [(CABLE, (0, 1), 4), (CABLE, (2, 3), 4)]
+)
 
 
 def bits(lo, n):
@@ -31,7 +32,7 @@ def owns(h, t):
 
 
 def engines(h, t):
-    return 4 if t in (8, 9) and not owns(h, t) else 2
+    return 2 if 16 <= t < 20 and not owns(h, t) else 1
 
 
 def dst_id(topo, dst, src):
@@ -46,20 +47,20 @@ def rank_side(g, core, T, topo):
     queues = ((g.sync, (0, 1)), (g.scalar, (2, 3)))
 
     def piece(j):
-        return slice(2 * j, 2 * j + 2), slice(32 * j, 32 * j + 32)
+        return slice(4 * j, 4 * j + 4), slice(32 * j, 32 * j + 32)
 
     for q, js in queues:
         for j in js:
-            if not owns(h, 2 * j):
+            if not owns(h, 4 * j):
                 sl, rows = piece(j)
                 q.dma_start(T.a[sl], T.x3[rows, :]).then_inc(s.ld1, 16)
-    g.sync.dma_start(T.a[8:10], T.x1[:]).then_inc(s.ld2, 16)
-    g.scalar.dma_start(T.a[10, 0:64, :], T.x4[:]).then_inc(s.ld2, 16)
-    g.scalar.dma_start(T.a[10, 64:66, :], T.x2[:]).then_inc(s.ld2, 16)
-    g.sync.dma_start(T.a[10, 66:128, :], T.x1[0:31, :]).then_inc(s.ld2, 16)
+    g.sync.dma_start(T.a[16:20], T.x1[:]).then_inc(s.ld2, 16)
+    g.scalar.dma_start(T.a[20], T.x4[:]).then_inc(s.ld2, 16)
+    g.scalar.dma_start(T.a[21, 0:4, :], T.x2[:]).then_inc(s.ld2, 16)
+    g.sync.dma_start(T.a[21, 4:128, :], T.x1[0:31, :]).then_inc(s.ld2, 16)
     for q, js in queues:
         for j in js:
-            if owns(h, 2 * j):
+            if owns(h, 4 * j):
                 sl, rows = piece(j)
                 q.dma_start(T.a[sl], T.x3[rows, :]).then_inc(s.ld2, 16)
 
@@ -73,25 +74,25 @@ def rank_side(g, core, T, topo):
                                  dma_engine_mask=bits(lo, n), remote_sem=s.s1, src=T.a[t], dst=T.b[t], alu_op=0)
 
     g.wait_ge(s.ld1, 32)
-    g.remote_dma_fused([hand(t, 2 * i) for i, t in enumerate(t for t in range(8) if not owns(h, t))], local_sem=s.ls)
+    g.remote_dma_fused([hand(t, i) for i, t in enumerate(t for t in range(NX) if not owns(h, t))], local_sem=s.ls)
     g.wait_ge(s.ld2, 96)
-    trs = [hand(t, 8 + 2 * i) for i, t in enumerate(t for t in range(8) if owns(h, t))]
+    trs = [hand(t, 8 + i) for i, t in enumerate(t for t in range(NX) if owns(h, t))]
     lo = 0
-    for t in (8, 9, 10):
+    for t in range(NX, NSLOT):
         trs.append(hand(t, lo))
         lo += engines(h, t)
     g.remote_dma_fused(trs, local_sem=s.ls)
 
     for q, js in queues:
-        for j in sorted(js, key=lambda j: not owns(h, 2 * j)):
+        for j in sorted(js, key=lambda j: not owns(h, 4 * j)):
             sl, rows = piece(j)
             q.wait_ge(s["r%d" % j], 16)
             q.dma_start(T.y3[rows, :], T.c[sl]).then_inc(s.st, 16)
-    g.sync.wait_ge(s.rs, 24)
-    g.sync.dma_start(T.y1[:], T.c[8:10]).then_inc(s.st, 16)
-    g.scalar.wait_ge(s.rs, 24)
-    g.scalar.dma_start(T.y4[:], T.c[10, 0:64, :]).then_inc(s.st, 16)
-    g.scalar.dma_start(T.y2[:], T.c[10, 64:66, :]).then_inc(s.st, 16)
+    g.sync.wait_ge(s.rs, 48)
+    g.sync.dma_start(T.y1[:], T.c[16:20]).then_inc(s.st, 16)
+    g.scalar.wait_ge(s.rs, 48)
+    g.scalar.dma_start(T.y4[:], T.c[20]).then_inc(s.st, 16)
+    g.scalar.dma_start(T.y2[:], T.c[21, 0:4, :]).then_inc(s.st, 16)
     g.wait_ge(s.ls, 8 + 8 + 8)
     g.wait_ge(s.st, 7 * 16)
 
@@ -103,21 +104,24 @@ def helper_side(g, core, T, topo):
     mine = [t for t in range(NSLOT) if SLOTS[t][2] == k and owns(h, t)]
     if not mine:
         return
-    t = mine[0]
-    kind = SLOTS[t][0]
+    kind = SLOTS[mine[0]][0]
     first, second = partner(h, kind), partner(h, 1 - kind)
-    g.wait_ge(s.s1, engines(h, t) + engines(first, t))
+    e = 8 // len(mine)
+    g.wait_ge(s.s1, sum(engines(h, t) + engines(first, t) for t in mine))
     peer = dst_id(topo, second * 128 + core % 128, core)
-    g.remote_dma_fused([RemoteDMATransfer(dst_ids=[peer], dma_engine_mask=bits(0, 8), remote_sem=s.s2,
-                                          srcs=[T.a[t], T.b[t]], dsts=[T.c[t]], alu_op=1)], local_sem=s.ls)
+    g.remote_dma_fused([RemoteDMATransfer(dst_ids=[peer], dma_engine_mask=bits(i * e, e), remote_sem=s.s2,
+                                          srcs=[T.a[t], T.b[t]], dsts=[T.c[t]], alu_op=1)
+                        for i, t in enumerate(mine)], local_sem=s.ls)
     g.wait_ge(s.s2, 8)
     home = dst_id(topo, core - k + RANK_CORE, core)
     away = dst_id(topo, first * 128 + core % 128 - k + RANK_CORE, core)
-    done = s.rs if t >= 8 else s["r%d" % (t // 2)]
-    g.remote_dma_fused([RemoteDMATransfer(dst_ids=[away], dma_engine_mask=bits(0, 8), remote_sem=done,
-                                          srcs=[T.a[t], T.b[t], T.c[t]], dsts=[T.c[t]], alu_op=1),
-                        RemoteDMATransfer(dst_ids=[home], dma_engine_mask=bits(8, 8), remote_sem=done,
-                                          srcs=[T.a[t], T.b[t], T.c[t]], dsts=[T.c[t]], alu_op=1)], local_sem=s.ls)
+    done = s.rs if mine[0] >= NX else s["r%d" % (mine[0] // 4)]
+    trs = []
+    for lo, dst in ((0, away), (8, home)):
+        for i, t in enumerate(mine):
+            trs.append(RemoteDMATransfer(dst_ids=[dst], dma_engine_mask=bits(lo + i * e, e), remote_sem=done,
+                                         srcs=[T.a[t], T.b[t], T.c[t]], dsts=[T.c[t]], alu_op=1))
+    g.remote_dma_fused(trs, local_sem=s.ls)
     g.wait_ge(s.ls, 24)
 
 

from concourse.bass import DstId, RemoteDMATransfer

NSLOT = 22
SCRATCH = {
    "a": ("dram", [NSLOT, 128, 32], "float32"),
    "b": ("dram", [NSLOT, 128, 32], "float32"),
    "c": ("dram", [NSLOT, 128, 32], "float32"),
}
SEMAPHORES = ["ld1", "ld2", "s1", "s2", "ls", "r0", "r1", "r2", "r3", "rs", "st"]

RACK, CABLE = 0, 1
RANK_CORE = 5
NX = 16
SLOTS = (
    [(RACK, (0, 3), 0)] * 2 + [(RACK, (0, 3), 6)] * 2 + [(RACK, (1, 2), 0)] * 2 + [(RACK, (1, 2), 6)] * 2
    + [(CABLE, (0, 1), 1)] * 2 + [(CABLE, (0, 1), 7)] * 2 + [(CABLE, (2, 3), 1)] * 2 + [(CABLE, (2, 3), 7)] * 2
    + [(RACK, (0, 3), 2), (RACK, (1, 2), 2), (CABLE, (0, 1), 3), (CABLE, (2, 3), 3)]
    + [(CABLE, (0, 1), 4), (CABLE, (2, 3), 4)]
)


def bits(lo, n):
    return ((1 << n) - 1) << lo


def partner(h, kind):
    return h ^ 1 if kind == RACK else 3 - h


def owns(h, t):
    return h in SLOTS[t][1]


def engines(h, t):
    return 2 if 16 <= t < 20 and not owns(h, t) else 1


def dst_id(topo, dst, src):
    rid, pid = topo.addr(dst, src)
    return DstId(rid=rid, pnc=pid)


def rank_side(g, core, T, topo):
    s = T.sem
    h = topo.host(core)
    chip0 = core % 128 - core % 8
    queues = ((g.sync, (0, 1)), (g.scalar, (2, 3)))

    def piece(j):
        return slice(4 * j, 4 * j + 4), slice(32 * j, 32 * j + 32)

    for q, js in queues:
        for j in js:
            if not owns(h, 4 * j):
                sl, rows = piece(j)
                q.dma_start(T.a[sl], T.x3[rows, :]).then_inc(s.ld1, 16)
    g.sync.dma_start(T.a[16:20], T.x1[:]).then_inc(s.ld2, 16)
    g.scalar.dma_start(T.a[20], T.x4[:]).then_inc(s.ld2, 16)
    g.scalar.dma_start(T.a[21, 0:4, :], T.x2[:]).then_inc(s.ld2, 16)
    g.sync.dma_start(T.a[21, 4:128, :], T.x1[0:31, :]).then_inc(s.ld2, 16)
    for q, js in queues:
        for j in js:
            if owns(h, 4 * j):
                sl, rows = piece(j)
                q.dma_start(T.a[sl], T.x3[rows, :]).then_inc(s.ld2, 16)

    def hand(t, lo):
        kind, owners, k = SLOTS[t]
        n = engines(h, t)
        if owns(h, t):
            return RemoteDMATransfer(dst_ids=[dst_id(topo, h * 128 + chip0 + k, core)], dma_engine_mask=bits(lo, n),
                                     remote_sem=s.s1, src=T.a[t], dst=T.a[t], alu_op=0)
        return RemoteDMATransfer(dst_ids=[dst_id(topo, partner(h, kind) * 128 + chip0 + k, core)],
                                 dma_engine_mask=bits(lo, n), remote_sem=s.s1, src=T.a[t], dst=T.b[t], alu_op=0)

    g.wait_ge(s.ld1, 32)
    g.remote_dma_fused([hand(t, i) for i, t in enumerate(t for t in range(NX) if not owns(h, t))], local_sem=s.ls)
    g.wait_ge(s.ld2, 96)
    trs = [hand(t, 8 + i) for i, t in enumerate(t for t in range(NX) if owns(h, t))]
    lo = 0
    for t in range(NX, NSLOT):
        trs.append(hand(t, lo))
        lo += engines(h, t)
    g.remote_dma_fused(trs, local_sem=s.ls)

    for q, js in queues:
        for j in sorted(js, key=lambda j: not owns(h, 4 * j)):
            sl, rows = piece(j)
            q.wait_ge(s["r%d" % j], 16)
            q.dma_start(T.y3[rows, :], T.c[sl]).then_inc(s.st, 16)
    g.sync.wait_ge(s.rs, 48)
    g.sync.dma_start(T.y1[:], T.c[16:20]).then_inc(s.st, 16)
    g.scalar.wait_ge(s.rs, 48)
    g.scalar.dma_start(T.y4[:], T.c[20]).then_inc(s.st, 16)
    g.scalar.dma_start(T.y2[:], T.c[21, 0:4, :]).then_inc(s.st, 16)
    g.wait_ge(s.ls, 8 + 8 + 8)
    g.wait_ge(s.st, 7 * 16)


def helper_side(g, core, T, topo):
    s = T.sem
    h = topo.host(core)
    k = core % 8
    mine = [t for t in range(NSLOT) if SLOTS[t][2] == k and owns(h, t)]
    if not mine:
        return
    kind = SLOTS[mine[0]][0]
    first, second = partner(h, kind), partner(h, 1 - kind)
    e = 8 // len(mine)
    g.wait_ge(s.s1, sum(engines(h, t) + engines(first, t) for t in mine))
    peer = dst_id(topo, second * 128 + core % 128, core)
    g.remote_dma_fused([RemoteDMATransfer(dst_ids=[peer], dma_engine_mask=bits(i * e, e), remote_sem=s.s2,
                                          srcs=[T.a[t], T.b[t]], dsts=[T.c[t]], alu_op=1)
                        for i, t in enumerate(mine)], local_sem=s.ls)
    g.wait_ge(s.s2, 8)
    home = dst_id(topo, core - k + RANK_CORE, core)
    away = dst_id(topo, first * 128 + core % 128 - k + RANK_CORE, core)
    done = s.rs if mine[0] >= NX else s["r%d" % (mine[0] // 4)]
    trs = []
    for lo, dst in ((0, away), (8, home)):
        for i, t in enumerate(mine):
            trs.append(RemoteDMATransfer(dst_ids=[dst], dma_engine_mask=bits(lo + i * e, e), remote_sem=done,
                                         srcs=[T.a[t], T.b[t], T.c[t]], dsts=[T.c[t]], alu_op=1))
    g.remote_dma_fused(trs, local_sem=s.ls)
    g.wait_ge(s.ls, 24)


def rank_program(g, core, T, topo):
    if T.rank_of(core) is not None:
        rank_side(g, core, T, topo)
    elif topo.chip(core) == topo.chip(T.cores[0]):
        helper_side(g, core, T, topo)
